import numpy as np
import ml_dtypes


def mxq(x, axis, fmt="e4m3"):
    dtype, down = {"e4m3": (ml_dtypes.float8_e4m3fn, 7), "e5m2": (ml_dtypes.float8_e5m2, 14)}[fmt]
    v = np.moveaxis(np.asarray(x, np.float32).astype(ml_dtypes.bfloat16).astype(np.float64), axis, -1)
    blocks = v.reshape(v.shape[:-1] + (-1, 32))
    amax = np.abs(blocks).max(-1, keepdims=True)
    byte = np.maximum(np.where(amax > 0, np.frexp(amax)[1] - 1 + 127, 0) - down, 1)
    scale = np.exp2(byte - 127.0)
    codes = (blocks / scale).astype(np.float32).astype(dtype).astype(np.float64)
    return np.moveaxis((codes * scale).reshape(v.shape), -1, axis)


WIDE = False


def mx_kscale(k):
    if not WIDE:
        return np.ones(k)
    levels = np.array([30, -30])
    if k % 512:
        return np.exp2(np.random.permutation(np.resize(levels, k // 32))).repeat(32)
    a = np.empty((k // 512, 16))
    for p in range(k // 512):
        a[p, :8] = np.random.permutation(np.resize(levels, 8))
        for g in range(8):
            far = levels[np.abs(levels - a[p, g]) >= 10]
            a[p, g + 8] = far[np.random.randint(len(far))]
    return np.exp2(a.ravel()).repeat(32)


def f64(x):
    return np.asarray(x).astype(np.float64)


def striped(idx):
    return np.tile(np.asarray(idx).reshape(-1, 16).T, (8, 1)).astype(np.uint16)


def unstriped(offs):
    return offs[:16].T.reshape(-1).astype(np.int64)


E2M1 = np.array([0.0, 0.5, 1.0, 1.5, 2.0, 3.0, 4.0, 6.0, -0.0, -0.5, -1.0, -1.5, -2.0, -3.0, -4.0, -6.0])


def pack_weight(w, fmt):
    k, n = w.shape
    w = f64(np.asarray(w, np.float32).astype(ml_dtypes.bfloat16)).reshape(k // 32, 32, n)
    amax = np.abs(w).max(1)
    if fmt == "e4m3":
        byte = np.frexp(amax)[1] - 1 + 127 - 7
    else:
        mant, ex = np.frexp(amax / 6.0)
        byte = np.where(mant > 0.5, ex, ex - 1) + 127
    byte = np.clip(np.where(amax > 0, byte, 1), 1, 254)
    scaled = (w * np.exp2(127.0 - byte)[:, None, :]).reshape(k, n).astype(np.float32)
    by_word = np.ascontiguousarray(scaled.reshape(k // 512, 128, 4, n).transpose(0, 1, 3, 2))
    if fmt == "e4m3":
        words = by_word.astype(ml_dtypes.float8_e4m3fn).view(np.uint8)
    else:
        c = by_word.astype(ml_dtypes.float4_e2m1fn).view(np.uint8) & 0xF
        words = (c[..., 0::2] | (c[..., 1::2] << 4)).reshape(k // 512, 128, 2 * n)
    return np.ascontiguousarray(words), np.ascontiguousarray(byte.astype(np.uint8).reshape(k // 512, 16, n))


def unpack_weight(words, scales, fmt):
    g, _, n = scales.shape
    words = np.ascontiguousarray(words).reshape(g, 128, n, -1)
    if fmt == "e4m3":
        vals = words.view(ml_dtypes.float8_e4m3fn).astype(np.float64)
    else:
        nib = np.empty((g, 128, n, 4), np.uint8)
        nib[..., 0::2] = words & 0xF
        nib[..., 1::2] = words >> 4
        vals = E2M1[nib]
    vals = vals * np.repeat(np.exp2(scales.astype(np.float64) - 127.0), 8, axis=1)[..., None]
    return vals.transpose(0, 1, 3, 2).reshape(g * 512, n)


K, T, Z, J, R, C, O, N, L, E = 512, 1024, 1024, 256, 512, 512, 256, 256, 512, 1024


def setup_inputs():
    n = np.random.standard_normal
    idx = np.random.permutation(T)[:J]
    idx2 = np.random.permutation(Z)[:J]
    idx3 = np.random.permutation(C)[:J]
    idx4 = np.random.permutation(C)[:J]
    idx5 = np.random.permutation(C)[:O]
    idx6 = np.random.permutation(C)[:O]
    idx7 = np.random.permutation(E)[:O]
    fk = mx_kscale(K)
    fr = mx_kscale(R)
    fl = mx_kscale(L)
    xtp = pack_weight(n((K, T)) / fk[:, None], "e2m1")
    xop = pack_weight(n((K, Z)) / fk[:, None], "e4m3")
    wp = pack_weight(n((K, R)) * 1 / np.sqrt(K) * fk[:, None] * fr, "e4m3")
    wbp = pack_weight(n((R, N)) * 1 / np.sqrt(R) / fr[:, None], "e2m1")
    sxp = pack_weight(n((L, O)) / fl[:, None], "e4m3")
    wsp = pack_weight(n((L, N)) * 1 / np.sqrt(L) * fl[:, None], "e4m3")
    return {
        "xt_words": xtp[0],
        "xt_scales": xtp[1],
        "xo_words": xop[0],
        "xo_scales": xop[1],
        "w_words": wp[0],
        "w_scales": wp[1],
        "wb_words": wbp[0],
        "wb_scales": wbp[1],
        "sx_words": sxp[0],
        "sx_scales": sxp[1],
        "ws_words": wsp[0],
        "ws_scales": wsp[1],
        "offs": striped(idx),
        "offs2": striped(idx2),
        "offs3": striped(idx3),
        "offs4": striped(idx4),
        "offs5": striped(idx5),
        "offs6": striped(idx6),
        "offs7": striped(idx7),
    }


def reference(xt_words, xt_scales, xo_words, xo_scales, w_words, w_scales, wb_words, wb_scales, sx_words, sx_scales, ws_words, ws_scales, offs, offs2, offs3, offs4, offs5, offs6, offs7):
    idx = unstriped(offs)
    idx2 = unstriped(offs2)
    idx3 = unstriped(offs3)
    idx4 = unstriped(offs4)
    idx5 = unstriped(offs5)
    idx6 = unstriped(offs6)
    idx7 = unstriped(offs7)
    xtu = unpack_weight(xt_words, xt_scales, "e2m1")
    xou = unpack_weight(xo_words, xo_scales, "e4m3")
    wu = unpack_weight(w_words, w_scales, "e4m3")
    wbu = unpack_weight(wb_words, wb_scales, "e2m1")
    sxu = unpack_weight(sx_words, sx_scales, "e4m3")
    wsu = unpack_weight(ws_words, ws_scales, "e4m3")
    xtidxg = xtu[:, idx]
    a = wu.T @ xtidxg
    xoidx2g = xou[:, idx2]
    b = wu.T @ xoidx2g
    pw = np.zeros((R, C))
    pw[:, idx3] = a
    pv = np.zeros((R, C))
    pv[:, idx4] = b
    hid = np.abs(pw[:, idx5] - pv[:, idx6])
    hidq = mxq(hid, 0, "e5m2")
    p = wbu.T @ hidq + wsu.T @ sxu
    y = np.zeros((N, E))
    y[:, idx7] = p
    return y

@@ -1,0 +1,217 @@
+from contextlib import ExitStack
+
+import concourse.mybir as mybir
+
+F32 = mybir.dt.float32
+BF16 = mybir.dt.bfloat16
+I32 = mybir.dt.int32
+U32 = mybir.dt.uint32
+U16 = mybir.dt.uint16
+U8 = mybir.dt.uint8
+E4M3 = mybir.dt.float8_e4m3fn_x4
+E5M2 = mybir.dt.float8_e5m2_x4
+E2M1 = mybir.dt.float4_e2m1fn_x4
+COPY = mybir.ActivationFunctionType.Copy
+ABS = mybir.ActivationFunctionType.Abs
+SUBTRACT = mybir.AluOpType.subtract
+
+P = 128
+PACK = 4
+TABLE = 1024
+SLOTS = 256
+HIDDEN = 512
+BOARD = 512
+READS = 256
+OUTF = 256
+PAGE = 1024
+HALF = READS // 2
+FLOPS = 2 * (2 * 512 * HIDDEN * SLOTS + 2 * 512 * OUTF * READS)
+
+
+def load_scale_rows(queue, plane, scales, quadrants):
+    for q in quadrants:
+        queue.dma_start(out=plane[32 * q : 32 * q + 4, :].bitcast(I32), in_=scales[0, 4 * q : 4 * q + 4, :].bitcast(I32))
+
+
+def as_words(words):
+    return words[0].rearrange("p n t -> p (n t)").bitcast(I32)
+
+
+def tile_list_oneforboth_twoboards_skip_scattered_kernel(
+    tc, xt_words, xt_scales, xo_words, xo_scales, w_words, w_scales, wb_words, wb_scales,
+    sx_words, sx_scales, ws_words, ws_scales, offs, offs2, offs3, offs4, offs5, offs6, offs7, out,
+):
+    nc = tc.nc
+    with ExitStack() as ctx:
+        lists = ctx.enter_context(tc.tile_pool(name="lists", bufs=1))
+        sb = ctx.enter_context(tc.tile_pool(name="sb", bufs=1))
+        psum = ctx.enter_context(tc.psum_pool(name="psum", bufs=1))
+
+        def list_tile(name):
+            return lists.tile([P, SLOTS // 16], U16, name=name)
+
+        l_tok = list_tile("l_tok")
+        l_note = list_tile("l_note")
+        l_put_a = list_tile("l_put_a")
+        l_put_b = list_tile("l_put_b")
+        l_get_a = list_tile("l_get_a")
+        l_get_b = list_tile("l_get_b")
+        l_page = list_tile("l_page")
+
+        xt_w = sb.tile([P, TABLE], U16, name="xt_w")
+        xt_s = sb.tile([P, TABLE], U8, name="xt_s")
+        xo_w = sb.tile([P, TABLE], U32, name="xo_w", tag="late0")
+        xo_s = sb.tile([P, TABLE], U8, name="xo_s", tag="late1")
+        w_raw = sb.tile([P, HIDDEN], U32, name="w_raw")
+        w_raw_s = sb.tile([P, HIDDEN], U8, name="w_raw_s")
+        w_w = sb.tile([P, HIDDEN], U32, name="w_w", align_bytes=64)
+        w_s = sb.tile([P, HIDDEN], U8, name="w_s", align_bytes=64)
+        wb_w = sb.tile([P, 2 * OUTF], U8, name="wb_w", align_bytes=64)
+        ws_w = sb.tile([P, OUTF], U32, name="ws_w", align_bytes=64)
+        sx_w = sb.tile([P, READS], U32, name="sx_w", align_bytes=64)
+        planes2 = sb.tile([P, 2 * OUTF + READS], U8, name="planes2", align_bytes=64)
+        wb_s = planes2[:, 0:OUTF]
+        ws_s = planes2[:, OUTF : 2 * OUTF]
+        sx_s = planes2[:, 2 * OUTF :]
+        board_a = [sb.tile([P, BOARD], F32, name="board_a%d" % t) for t in range(PACK)]
+        board_b = [sb.tile([P, BOARD], F32, name="board_b%d" % t) for t in range(PACK)]
+
+        nc.gpsimd.memset(xt_s[:].bitcast(I32), 0)
+        nc.gpsimd.memset(w_raw_s[:].bitcast(I32), 0)
+        nc.gpsimd.memset(xo_s[:].bitcast(I32), 0)
+        nc.gpsimd.memset(planes2[:].bitcast(I32), 0)
+
+        nc.sync.dma_start(l_tok[:], offs)
+        nc.scalar.dma_start(out=xt_w[:].bitcast(I32), in_=xt_words[0].bitcast(I32))
+        nc.sync.dma_start(out=w_raw[:].bitcast(I32), in_=as_words(w_words))
+        load_scale_rows(nc.scalar, xt_s, xt_scales, range(4))
+        load_scale_rows(nc.sync, w_raw_s, w_scales, range(4))
+        nc.sync.dma_start(l_put_a[:], offs3)
+        nc.sync.dma_start(l_note[:], offs2)
+        load_scale_rows(nc.sync, xo_s, xo_scales, range(4))
+        nc.sync.dma_start(out=xo_w[:].bitcast(I32), in_=as_words(xo_words))
+        nc.sync.dma_start(l_get_a[:], offs5)
+        nc.sync.dma_start(l_put_b[:], offs4)
+        nc.sync.dma_start(l_get_b[:], offs6)
+        nc.sync.dma_start(out=ws_w[:].bitcast(I32), in_=as_words(ws_words))
+        nc.sync.dma_start(out=sx_w[:].bitcast(I32), in_=as_words(sx_words))
+        nc.sync.dma_start(out=wb_w[:].bitcast(I32), in_=wb_words[0].bitcast(I32))
+        load_scale_rows(nc.sync, ws_s, ws_scales, range(4))
+        load_scale_rows(nc.sync, sx_s, sx_scales, range(4))
+        load_scale_rows(nc.sync, wb_s, wb_scales, range(4))
+        nc.sync.dma_start(l_page[:], offs7)
+
+        tok_w = sb.tile([P, SLOTS], U16, name="tok_w", align_bytes=64)
+        tok_s = sb.tile([P, SLOTS], U8, name="tok_s", align_bytes=64)
+        note_w = sb.tile([P, SLOTS], U32, name="note_w", align_bytes=64)
+        note_s = sb.tile([P, SLOTS], U8, name="note_s", align_bytes=64)
+
+        nc.vector.tensor_copy(tok_w[:], xt_w[:].indirect(l_tok[:]))
+        nc.vector.tensor_copy(tok_s[:], xt_s[:].indirect(l_tok[:]))
+        nc.vector.tensor_copy(
+            w_w[:].rearrange("p (t c i) -> p c t i", t=PACK, i=4),
+            w_raw[:].rearrange("p (c i t) -> p c t i", t=PACK, i=4),
+        )
+        nc.vector.tensor_copy(
+            w_s[:].rearrange("p (t c i) -> p c t i", t=PACK, i=16),
+            w_raw_s[:].rearrange("p (c i t) -> p c t i", t=PACK, i=16),
+        )
+        nc.vector.tensor_copy(note_w[:], xo_w[:].indirect(l_note[:]))
+        nc.vector.tensor_copy(note_s[:], xo_s[:].indirect(l_note[:]))
+
+        for t in range(PACK):
+            nc.vector.memset(board_a[t][:], 0.0)
+        for t in range(PACK):
+            nc.vector.memset(board_b[t][:], 0.0)
+
+        def first_stage(acc, t, words, plane):
+            cols = slice(P * t, P * (t + 1))
+            nc.tensor.matmul_mx(
+                out=acc, lhsT=w_w[:, cols].bitcast(E4M3), lhsT_scale=w_s[:, cols],
+                rhs=words, rhs_scale=plane, start=True, stop=True,
+            )
+
+        acc_a0 = psum.tile([P, SLOTS], F32, name="acc_a0", tag="bank0")
+        acc_b0 = psum.tile([P, SLOTS], F32, name="acc_b0", tag="bank1")
+        acc_ab = [psum.tile([P, 2, SLOTS], F32, name="acc_ab%d" % t) for t in range(1, PACK)]
+        acc_a = [acc_a0[:]] + [acc[:, 0, :] for acc in acc_ab]
+        acc_b = [acc_b0[:]] + [acc[:, 1, :] for acc in acc_ab]
+        for t in range(PACK):
+            first_stage(acc_a[t], t, tok_w[:].bitcast(E2M1), tok_s[:])
+        for t in range(PACK):
+            first_stage(acc_b[t], t, note_w[:].bitcast(E4M3), note_s[:])
+
+        pages = [sb.tile([P, PAGE], F32, name="page%d" % g, tag="late%d" % g) for g in range(2)]
+        for g in range(2):
+            nc.gpsimd.memset(pages[g][:], 0.0)
+
+        a0_sb = sb.tile([P, SLOTS], F32, name="a0_sb")
+        b0_sb = sb.tile([P, SLOTS], F32, name="b0_sb")
+        ab_sb = [
+            sb.tile([P, 2, SLOTS], F32, name="ab_sb%d" % t, tag="ab_sb%d" % t, align_bytes=64) for t in range(1, PACK)
+        ]
+        a_sb = [a0_sb[:]] + [x[:, 0, :] for x in ab_sb]
+        b_sb = [b0_sb[:]] + [x[:, 1, :] for x in ab_sb]
+        nc.scalar.activation(a0_sb[:], acc_a0[:], COPY)
+        nc.vector.tensor_copy(b0_sb[:], acc_b0[:])
+
+        acc_p = [
+            [psum.tile([P, HALF], F32, name="acc_p%d%d" % (g, h), tag="bank%d" % (2 * h + g)) for h in range(2)]
+            for g in range(2)
+        ]
+        for h in range(2):
+            for g in range(2):
+                cols = slice(P * g, P * (g + 1))
+                reads = slice(HALF * h, HALF * (h + 1))
+                nc.tensor.matmul_mx(
+                    out=acc_p[g][h][:], lhsT=ws_w[:, cols].bitcast(E4M3), lhsT_scale=ws_s[:, cols],
+                    rhs=sx_w[:, reads].bitcast(E4M3), rhs_scale=sx_s[:, reads], start=True, stop=False,
+                )
+
+        diff_lo = sb.tile([P, 2, READS], F32, name="diff_lo")
+        diff_hi = [sb.tile([P, 2, HALF], F32, name="diff_hi%d" % h) for h in range(2)]
+        for t in range(PACK):
+            if t > 0:
+                nc.scalar.activation(ab_sb[t - 1][:], acc_ab[t - 1][:], COPY)
+            nc.scalar.activation(board_a[t][:].indirect(l_put_a[:]), a_sb[t], COPY)
+            nc.vector.tensor_copy(board_b[t][:].indirect(l_put_b[:]), b_sb[t])
+            if t < 2:
+                got_a = sb.tile([P, READS], F32, name="got_a%d" % t)
+                nc.scalar.activation(got_a[:], board_a[t][:].indirect(l_get_a[:]), COPY)
+                nc.vector.tensor_tensor(diff_lo[:, t, :], board_b[t][:].indirect(l_get_b[:]), got_a[:], SUBTRACT)
+            else:
+                for h in range(2):
+                    part = slice(HALF // 16 * h, HALF // 16 * (h + 1))
+                    got_a = sb.tile([P, HALF], F32, name="got_a%d%d" % (t, h), tag="got_a%d%d" % (t, h), align_bytes=64)
+                    nc.scalar.activation(got_a[:], board_a[t][:].indirect(l_get_a[:, part]), COPY)
+                    nc.vector.tensor_tensor(
+                        diff_hi[h][:, t - 2, :], board_b[t][:].indirect(l_get_b[:, part]), got_a[:], SUBTRACT
+                    )
+
+        hid_w = []
+        hid_s = []
+        for h, tag in enumerate(("ab_sb3", "got_a30")):
+            reads = slice(HALF * h, HALF * (h + 1))
+            hid = sb.tile([P, HALF, PACK], BF16, name="hid%d" % h, tag=tag, align_bytes=64)
+            hid_w.append(sb.tile([P, HALF], U32, name="hid_w%d" % h, align_bytes=64))
+            hid_s.append(sb.tile([P, HALF], U8, name="hid_s%d" % h, align_bytes=64))
+            nc.scalar.activation(hid[:, :, 0:2], diff_lo[:, :, reads].rearrange("p e o -> p o e"), ABS)
+            nc.scalar.activation(hid[:, :, 2:4], diff_hi[h][:].rearrange("p e o -> p o e"), ABS)
+            nc.vector.quantize_mx(out=hid_w[h][:].bitcast(E5M2), scales=hid_s[h][:], in_=hid[:].rearrange("p o t -> p (o t)"))
+
+        for h in range(2):
+            for g in range(2):
+                nc.tensor.matmul_mx(
+                    out=acc_p[g][h][:], lhsT=wb_w[:, 2 * P * g : 2 * P * (g + 1)].bitcast(E2M1),
+                    lhsT_scale=wb_s[:, P * g : P * (g + 1)],
+                    rhs=hid_w[h][:].bitcast(E5M2), rhs_scale=hid_s[h][:], start=False, stop=True,
+                )
+        for h in range(2):
+            part = slice(HALF // 16 * h, HALF // 16 * (h + 1))
+            p_sb = [sb.tile([P, HALF], F32, name="p_sb%d%d" % (g, h)) for g in range(2)]
+            nc.scalar.activation(p_sb[0][:], acc_p[0][h][:], COPY)
+            nc.scalar.activation(pages[0][:].indirect(l_page[:, part]), p_sb[0][:], COPY)
+            nc.vector.tensor_copy(p_sb[1][:], acc_p[1][h][:])
+            nc.vector.tensor_copy(pages[1][:].indirect(l_page[:, part]), p_sb[1][:])
+        nc.scalar.dma_start(out=out[0:P, :], in_=pages[0][:])
+        nc.sync.dma_start(out=out[P : 2 * P, :], in_=pages[1][:])

@@ -30,7 +30,8 @@ FLOPS = 2 * (2 * 512 * HIDDEN * SLOTS + 2 * 512 * OUTF * READS)
 
 def load_scale_rows(queue, plane, scales, quadrants):
     for q in quadrants:
-        queue.dma_start(out=plane[32 * q : 32 * q + 4, :].bitcast(I32), in_=scales[0, 4 * q : 4 * q + 4, :].bitcast(I32))
+        rows = scales[0, 4 * q : 4 * q + 4, :].bitcast(I32)
+        queue.dma_start(out=plane[32 * q : 32 * q + 32, :].bitcast(I32), in_=rows.partition_broadcast(8))
 
 
 def as_words(words):
@@ -65,7 +66,9 @@ def tile_list_oneforboth_twoboards_skip_scattered_kernel(
         w_raw = sb.tile([P, HIDDEN], U32, name="w_raw")
         w_raw_s = sb.tile([P, HIDDEN], U8, name="w_raw_s")
         w_w = sb.tile([P, HIDDEN], U32, name="w_w", align_bytes=64)
-        w_s = sb.tile([P, HIDDEN], U8, name="w_s", align_bytes=64)
+        w_s0 = sb.tile([P, P], U8, name="w_s0", align_bytes=64)
+        w_s123 = sb.tile([P, HIDDEN - P], U8, name="w_s123", tag="then_board3", align_bytes=64)
+        w_s = [w_s0[:]] + [w_s123[:, P * t : P * (t + 1)] for t in range(PACK - 1)]
         wb_w = sb.tile([P, 2 * OUTF], U8, name="wb_w", align_bytes=64)
         ws_w = sb.tile([P, OUTF], U32, name="ws_w", align_bytes=64)
         sx_w = sb.tile([P, READS], U32, name="sx_w", align_bytes=64)
@@ -74,24 +77,23 @@ def tile_list_oneforboth_twoboards_skip_scattered_kernel(
         ws_s = planes2[:, OUTF : 2 * OUTF]
         sx_s = planes2[:, 2 * OUTF :]
         board_a = [sb.tile([P, BOARD], F32, name="board_a%d" % t) for t in range(PACK)]
-        board_b = [sb.tile([P, BOARD], F32, name="board_b%d" % t) for t in range(PACK)]
 
-        nc.gpsimd.memset(xt_s[:].bitcast(I32), 0)
-        nc.gpsimd.memset(w_raw_s[:].bitcast(I32), 0)
-        nc.gpsimd.memset(xo_s[:].bitcast(I32), 0)
-        nc.gpsimd.memset(planes2[:].bitcast(I32), 0)
 
         nc.sync.dma_start(l_tok[:], offs)
-        nc.scalar.dma_start(out=xt_w[:].bitcast(I32), in_=xt_words[0].bitcast(I32))
+        load_scale_rows(nc.scalar, xt_s, xt_scales, (0,))
+        load_scale_rows(nc.sync, xt_s, xt_scales, (1,))
+        load_scale_rows(nc.scalar, xt_s, xt_scales, (2,))
+        nc.sync.dma_start(out=xt_w[:].bitcast(I32), in_=xt_words[0].bitcast(I32))
+        load_scale_rows(nc.scalar, xt_s, xt_scales, (3,))
         nc.sync.dma_start(out=w_raw[:].bitcast(I32), in_=as_words(w_words))
-        load_scale_rows(nc.scalar, xt_s, xt_scales, range(4))
+        nc.scalar.dma_start(out=xo_w[:].bitcast(I32), in_=as_words(xo_words))
         load_scale_rows(nc.sync, w_raw_s, w_scales, range(4))
-        nc.sync.dma_start(l_put_a[:], offs3)
+        load_scale_rows(nc.gpsimd, xo_s, xo_scales, (2, 3))
         nc.sync.dma_start(l_note[:], offs2)
-        load_scale_rows(nc.sync, xo_s, xo_scales, range(4))
-        nc.sync.dma_start(out=xo_w[:].bitcast(I32), in_=as_words(xo_words))
-        nc.sync.dma_start(l_get_a[:], offs5)
+        load_scale_rows(nc.sync, xo_s, xo_scales, (0, 1))
+        nc.sync.dma_start(l_put_a[:], offs3)
         nc.sync.dma_start(l_put_b[:], offs4)
+        nc.sync.dma_start(l_get_a[:], offs5)
         nc.sync.dma_start(l_get_b[:], offs6)
         nc.sync.dma_start(out=ws_w[:].bitcast(I32), in_=as_words(ws_words))
         nc.sync.dma_start(out=sx_w[:].bitcast(I32), in_=as_words(sx_words))
@@ -101,8 +103,8 @@ def tile_list_oneforboth_twoboards_skip_scattered_kernel(
         load_scale_rows(nc.sync, wb_s, wb_scales, range(4))
         nc.sync.dma_start(l_page[:], offs7)
 
-        tok_w = sb.tile([P, SLOTS], U16, name="tok_w", align_bytes=64)
-        tok_s = sb.tile([P, SLOTS], U8, name="tok_s", align_bytes=64)
+        tok_w = sb.tile([P, SLOTS], U16, name="tok_w", tag="then_board1", align_bytes=64)
+        tok_s = sb.tile([P, SLOTS], U8, name="tok_s", tag="then_board2", align_bytes=64)
         note_w = sb.tile([P, SLOTS], U32, name="note_w", align_bytes=64)
         note_s = sb.tile([P, SLOTS], U8, name="note_s", align_bytes=64)
 
@@ -112,48 +114,52 @@ def tile_list_oneforboth_twoboards_skip_scattered_kernel(
             w_w[:].rearrange("p (t c i) -> p c t i", t=PACK, i=4),
             w_raw[:].rearrange("p (c i t) -> p c t i", t=PACK, i=4),
         )
-        nc.vector.tensor_copy(
-            w_s[:].rearrange("p (t c i) -> p c t i", t=PACK, i=16),
-            w_raw_s[:].rearrange("p (c i t) -> p c t i", t=PACK, i=16),
-        )
+        as_loaded = w_raw_s[:].rearrange("p (c i t) -> p c t i", t=PACK, i=16)
+        nc.vector.tensor_copy(w_s0[:].rearrange("p (c i) -> p c i", i=16), as_loaded[:, :, 0, :])
         nc.vector.tensor_copy(note_w[:], xo_w[:].indirect(l_note[:]))
         nc.vector.tensor_copy(note_s[:], xo_s[:].indirect(l_note[:]))
+        nc.vector.tensor_copy(w_s123[:].rearrange("p (t c i) -> p c t i", t=PACK - 1, i=16), as_loaded[:, :, 1:PACK, :])
 
         for t in range(PACK):
             nc.vector.memset(board_a[t][:], 0.0)
-        for t in range(PACK):
-            nc.vector.memset(board_b[t][:], 0.0)
+        board_b0 = sb.tile([P, BOARD], F32, name="board_b0")
+        nc.vector.memset(board_b0[:], 0.0)
 
         def first_stage(acc, t, words, plane):
             cols = slice(P * t, P * (t + 1))
             nc.tensor.matmul_mx(
-                out=acc, lhsT=w_w[:, cols].bitcast(E4M3), lhsT_scale=w_s[:, cols],
+                out=acc, lhsT=w_w[:, cols].bitcast(E4M3), lhsT_scale=w_s[t],
                 rhs=words, rhs_scale=plane, start=True, stop=True,
             )
 
-        acc_a0 = psum.tile([P, SLOTS], F32, name="acc_a0", tag="bank0")
-        acc_b0 = psum.tile([P, SLOTS], F32, name="acc_b0", tag="bank1")
-        acc_ab = [psum.tile([P, 2, SLOTS], F32, name="acc_ab%d" % t) for t in range(1, PACK)]
-        acc_a = [acc_a0[:]] + [acc[:, 0, :] for acc in acc_ab]
-        acc_b = [acc_b0[:]] + [acc[:, 1, :] for acc in acc_ab]
+        acc_a_lo = [psum.tile([P, SLOTS], F32, name="acc_a%d" % t, tag="bank%d" % t) for t in range(2)]
+        acc_b_lo = [psum.tile([P, SLOTS], F32, name="acc_b%d" % t) for t in range(2)]
+        acc_ab = [psum.tile([P, 2, SLOTS], F32, name="acc_ab%d" % t) for t in range(2, PACK)]
+        acc_a = [acc[:] for acc in acc_a_lo] + [acc[:, 0, :] for acc in acc_ab]
+        acc_b = [acc[:] for acc in acc_b_lo] + [acc[:, 1, :] for acc in acc_ab]
         for t in range(PACK):
             first_stage(acc_a[t], t, tok_w[:].bitcast(E2M1), tok_s[:])
-        for t in range(PACK):
             first_stage(acc_b[t], t, note_w[:].bitcast(E4M3), note_s[:])
 
+        board_b = [board_b0] + [
+            sb.tile([P, BOARD], F32, name="board_b%d" % t, tag="then_board%d" % t, align_bytes=64) for t in range(1, PACK)
+        ]
+        for t in range(1, PACK):
+            nc.gpsimd.memset(board_b[t][:], 0.0)
         pages = [sb.tile([P, PAGE], F32, name="page%d" % g, tag="late%d" % g) for g in range(2)]
         for g in range(2):
             nc.gpsimd.memset(pages[g][:], 0.0)
 
-        a0_sb = sb.tile([P, SLOTS], F32, name="a0_sb")
-        b0_sb = sb.tile([P, SLOTS], F32, name="b0_sb")
+        a_lo_sb = [sb.tile([P, SLOTS], F32, name="a_sb%d" % t) for t in range(2)]
+        b_lo_sb = [sb.tile([P, SLOTS], F32, name="b_sb%d" % t) for t in range(2)]
         ab_sb = [
-            sb.tile([P, 2, SLOTS], F32, name="ab_sb%d" % t, tag="ab_sb%d" % t, align_bytes=64) for t in range(1, PACK)
+            sb.tile([P, 2, SLOTS], F32, name="ab_sb%d" % t, tag="ab_sb%d" % t, align_bytes=64) for t in range(2, PACK)
         ]
-        a_sb = [a0_sb[:]] + [x[:, 0, :] for x in ab_sb]
-        b_sb = [b0_sb[:]] + [x[:, 1, :] for x in ab_sb]
-        nc.scalar.activation(a0_sb[:], acc_a0[:], COPY)
-        nc.vector.tensor_copy(b0_sb[:], acc_b0[:])
+        a_sb = [x[:] for x in a_lo_sb] + [x[:, 0, :] for x in ab_sb]
+        b_sb = [x[:] for x in b_lo_sb] + [x[:, 1, :] for x in ab_sb]
+        for t in range(2):
+            nc.scalar.activation(a_sb[t], acc_a[t], COPY)
+            nc.vector.tensor_copy(b_sb[t], acc_b[t])
 
         acc_p = [
             [psum.tile([P, HALF], F32, name="acc_p%d%d" % (g, h), tag="bank%d" % (2 * h + g)) for h in range(2)]
@@ -171,8 +177,8 @@ def tile_list_oneforboth_twoboards_skip_scattered_kernel(
         diff_lo = sb.tile([P, 2, READS], F32, name="diff_lo")
         diff_hi = [sb.tile([P, 2, HALF], F32, name="diff_hi%d" % h) for h in range(2)]
         for t in range(PACK):
-            if t > 0:
-                nc.scalar.activation(ab_sb[t - 1][:], acc_ab[t - 1][:], COPY)
+            if t >= 2:
+                nc.scalar.activation(ab_sb[t - 2][:], acc_ab[t - 2][:], COPY)
             nc.scalar.activation(board_a[t][:].indirect(l_put_a[:]), a_sb[t], COPY)
             nc.vector.tensor_copy(board_b[t][:].indirect(l_put_b[:]), b_sb[t])
             if t < 2:
@@ -190,7 +196,7 @@ def tile_list_oneforboth_twoboards_skip_scattered_kernel(
 
         hid_w = []
         hid_s = []
-        for h, tag in enumerate(("ab_sb3", "got_a30")):
+        for h, tag in enumerate(("ab_sb3", "ab_sb2")):
             reads = slice(HALF * h, HALF * (h + 1))
             hid = sb.tile([P, HALF, PACK], BF16, name="hid%d" % h, tag=tag, align_bytes=64)
             hid_w.append(sb.tile([P, HALF], U32, name="hid_w%d" % h, align_bytes=64))

@@ -61,13 +61,13 @@ def tile_list_oneforboth_twoboards_skip_scattered_kernel(
 
         xt_w = sb.tile([P, TABLE], U16, name="xt_w")
         xt_s = sb.tile([P, TABLE], U8, name="xt_s")
-        xo_w = sb.tile([P, TABLE], U32, name="xo_w", tag="late0")
-        xo_s = sb.tile([P, TABLE], U8, name="xo_s", tag="late1")
+        xo_w = sb.tile([P, TABLE], U32, name="xo_w")
+        xo_s = sb.tile([P, TABLE], U8, name="xo_s")
         w_raw = sb.tile([P, HIDDEN], U32, name="w_raw")
         w_raw_s = sb.tile([P, HIDDEN], U8, name="w_raw_s")
         w_w = sb.tile([P, HIDDEN], U32, name="w_w", align_bytes=64)
         w_s0 = sb.tile([P, P], U8, name="w_s0", align_bytes=64)
-        w_s123 = sb.tile([P, HIDDEN - P], U8, name="w_s123", tag="then_board3", align_bytes=64)
+        w_s123 = sb.tile([P, HIDDEN - P], U8, name="w_s123", align_bytes=64)
         w_s = [w_s0[:]] + [w_s123[:, P * t : P * (t + 1)] for t in range(PACK - 1)]
         wb_w = sb.tile([P, 2 * OUTF], U8, name="wb_w", align_bytes=64)
         ws_w = sb.tile([P, OUTF], U32, name="ws_w", align_bytes=64)
@@ -77,6 +77,7 @@ def tile_list_oneforboth_twoboards_skip_scattered_kernel(
         ws_s = planes2[:, OUTF : 2 * OUTF]
         sx_s = planes2[:, 2 * OUTF :]
         board_a = [sb.tile([P, BOARD], F32, name="board_a%d" % t) for t in range(PACK)]
+        board_b = [sb.tile([P, BOARD], F32, name="board_b%d" % t) for t in range(PACK)]
 
 
         nc.sync.dma_start(l_tok[:], offs)
@@ -103,8 +104,8 @@ def tile_list_oneforboth_twoboards_skip_scattered_kernel(
         load_scale_rows(nc.sync, wb_s, wb_scales, range(4))
         nc.sync.dma_start(l_page[:], offs7)
 
-        tok_w = sb.tile([P, SLOTS], U16, name="tok_w", tag="then_board1", align_bytes=64)
-        tok_s = sb.tile([P, SLOTS], U8, name="tok_s", tag="then_board2", align_bytes=64)
+        tok_w = sb.tile([P, SLOTS], U16, name="tok_w", align_bytes=64)
+        tok_s = sb.tile([P, SLOTS], U8, name="tok_s", align_bytes=64)
         note_w = sb.tile([P, SLOTS], U32, name="note_w", align_bytes=64)
         note_s = sb.tile([P, SLOTS], U8, name="note_s", align_bytes=64)
 
@@ -122,8 +123,9 @@ def tile_list_oneforboth_twoboards_skip_scattered_kernel(
 
         for t in range(PACK):
             nc.vector.memset(board_a[t][:], 0.0)
-        board_b0 = sb.tile([P, BOARD], F32, name="board_b0")
-        nc.vector.memset(board_b0[:], 0.0)
+            nc.vector.memset(board_b[t][:], 0.0)
+        page0 = sb.tile([P, PAGE], F32, name="page0")
+        nc.vector.memset(page0[:], 0.0)
 
         def first_stage(acc, t, words, plane):
             cols = slice(P * t, P * (t + 1))
@@ -140,15 +142,6 @@ def tile_list_oneforboth_twoboards_skip_scattered_kernel(
         for t in range(PACK):
             first_stage(acc_a[t], t, tok_w[:].bitcast(E2M1), tok_s[:])
             first_stage(acc_b[t], t, note_w[:].bitcast(E4M3), note_s[:])
-
-        board_b = [board_b0] + [
-            sb.tile([P, BOARD], F32, name="board_b%d" % t, tag="then_board%d" % t, align_bytes=64) for t in range(1, PACK)
-        ]
-        for t in range(1, PACK):
-            nc.gpsimd.memset(board_b[t][:], 0.0)
-        pages = [sb.tile([P, PAGE], F32, name="page%d" % g, tag="late%d" % g) for g in range(2)]
-        for g in range(2):
-            nc.gpsimd.memset(pages[g][:], 0.0)
 
         a_lo_sb = [sb.tile([P, SLOTS], F32, name="a_sb%d" % t) for t in range(2)]
         b_lo_sb = [sb.tile([P, SLOTS], F32, name="b_sb%d" % t) for t in range(2)]
@@ -205,6 +198,9 @@ def tile_list_oneforboth_twoboards_skip_scattered_kernel(
             nc.scalar.activation(hid[:, :, 2:4], diff_hi[h][:].rearrange("p e o -> p o e"), ABS)
             nc.vector.quantize_mx(out=hid_w[h][:].bitcast(E5M2), scales=hid_s[h][:], in_=hid[:].rearrange("p o t -> p (o t)"))
 
+        page1 = sb.tile([P, PAGE], F32, name="page1", tag="ab_sb3", align_bytes=64)
+        nc.vector.memset(page1[:], 0.0)
+        pages = [page0, page1]
         for h in range(2):
             for g in range(2):
                 nc.tensor.matmul_mx(

@@ -90,9 +90,9 @@ def tile_list_oneforboth_twoboards_skip_scattered_kernel(
         nc.scalar.dma_start(out=xo_w[:].bitcast(I32), in_=as_words(xo_words))
         load_scale_rows(nc.sync, w_raw_s, w_scales, range(4))
         load_scale_rows(nc.gpsimd, xo_s, xo_scales, (2, 3))
+        nc.sync.dma_start(l_put_a[:], offs3)
         nc.sync.dma_start(l_note[:], offs2)
         load_scale_rows(nc.sync, xo_s, xo_scales, (0, 1))
-        nc.sync.dma_start(l_put_a[:], offs3)
         nc.sync.dma_start(l_put_b[:], offs4)
         nc.sync.dma_start(l_get_a[:], offs5)
         nc.sync.dma_start(l_get_b[:], offs6)
@@ -117,9 +117,9 @@ def tile_list_oneforboth_twoboards_skip_scattered_kernel(
         )
         as_loaded = w_raw_s[:].rearrange("p (c i t) -> p c t i", t=PACK, i=16)
         nc.vector.tensor_copy(w_s0[:].rearrange("p (c i) -> p c i", i=16), as_loaded[:, :, 0, :])
+        nc.vector.tensor_copy(w_s123[:].rearrange("p (t c i) -> p c t i", t=PACK - 1, i=16), as_loaded[:, :, 1:PACK, :])
         nc.vector.tensor_copy(note_w[:], xo_w[:].indirect(l_note[:]))
         nc.vector.tensor_copy(note_s[:], xo_s[:].indirect(l_note[:]))
-        nc.vector.tensor_copy(w_s123[:].rearrange("p (t c i) -> p c t i", t=PACK - 1, i=16), as_loaded[:, :, 1:PACK, :])
 
         for t in range(PACK):
             nc.vector.memset(board_a[t][:], 0.0)
@@ -136,20 +136,20 @@ def tile_list_oneforboth_twoboards_skip_scattered_kernel(
 
         acc_a_lo = [psum.tile([P, SLOTS], F32, name="acc_a%d" % t, tag="bank%d" % t) for t in range(2)]
         acc_b_lo = [psum.tile([P, SLOTS], F32, name="acc_b%d" % t) for t in range(2)]
-        acc_ab = [psum.tile([P, 2, SLOTS], F32, name="acc_ab%d" % t) for t in range(2, PACK)]
-        acc_a = [acc[:] for acc in acc_a_lo] + [acc[:, 0, :] for acc in acc_ab]
-        acc_b = [acc[:] for acc in acc_b_lo] + [acc[:, 1, :] for acc in acc_ab]
+        acc_a_hi = psum.tile([P, 2, SLOTS], F32, name="acc_a_hi")
+        acc_b_hi = psum.tile([P, 2, SLOTS], F32, name="acc_b_hi")
+        acc_a = [acc[:] for acc in acc_a_lo] + [acc_a_hi[:, e, :] for e in range(2)]
+        acc_b = [acc[:] for acc in acc_b_lo] + [acc_b_hi[:, e, :] for e in range(2)]
         for t in range(PACK):
             first_stage(acc_a[t], t, tok_w[:].bitcast(E2M1), tok_s[:])
             first_stage(acc_b[t], t, note_w[:].bitcast(E4M3), note_s[:])
 
         a_lo_sb = [sb.tile([P, SLOTS], F32, name="a_sb%d" % t) for t in range(2)]
         b_lo_sb = [sb.tile([P, SLOTS], F32, name="b_sb%d" % t) for t in range(2)]
-        ab_sb = [
-            sb.tile([P, 2, SLOTS], F32, name="ab_sb%d" % t, tag="ab_sb%d" % t, align_bytes=64) for t in range(2, PACK)
-        ]
-        a_sb = [x[:] for x in a_lo_sb] + [x[:, 0, :] for x in ab_sb]
-        b_sb = [x[:] for x in b_lo_sb] + [x[:, 1, :] for x in ab_sb]
+        a_hi_sb = sb.tile([P, 2, SLOTS], F32, name="a_hi_sb", tag="a_hi", align_bytes=64)
+        b_hi_sb = sb.tile([P, 2, SLOTS], F32, name="b_hi_sb", tag="b_hi", align_bytes=64)
+        a_sb = [x[:] for x in a_lo_sb] + [a_hi_sb[:, e, :] for e in range(2)]
+        b_sb = [x[:] for x in b_lo_sb] + [b_hi_sb[:, e, :] for e in range(2)]
         for t in range(2):
             nc.scalar.activation(a_sb[t], acc_a[t], COPY)
             nc.vector.tensor_copy(b_sb[t], acc_b[t])
@@ -170,8 +170,9 @@ def tile_list_oneforboth_twoboards_skip_scattered_kernel(
         diff_lo = sb.tile([P, 2, READS], F32, name="diff_lo")
         diff_hi = [sb.tile([P, 2, HALF], F32, name="diff_hi%d" % h) for h in range(2)]
         for t in range(PACK):
-            if t >= 2:
-                nc.scalar.activation(ab_sb[t - 2][:], acc_ab[t - 2][:], COPY)
+            if t == 2:
+                nc.scalar.activation(a_hi_sb[:], acc_a_hi[:], COPY)
+                nc.vector.tensor_copy(b_hi_sb[:], acc_b_hi[:])
             nc.scalar.activation(board_a[t][:].indirect(l_put_a[:]), a_sb[t], COPY)
             nc.vector.tensor_copy(board_b[t][:].indirect(l_put_b[:]), b_sb[t])
             if t < 2:
@@ -181,15 +182,18 @@ def tile_list_oneforboth_twoboards_skip_scattered_kernel(
             else:
                 for h in range(2):
                     part = slice(HALF // 16 * h, HALF // 16 * (h + 1))
-                    got_a = sb.tile([P, HALF], F32, name="got_a%d%d" % (t, h), tag="got_a%d%d" % (t, h), align_bytes=64)
-                    nc.scalar.activation(got_a[:], board_a[t][:].indirect(l_get_a[:, part]), COPY)
+                    got_a = sb.tile([P, HALF], F32, name="got_a%d%d" % (t, h))
+                    if t == 2:
+                        nc.vector.tensor_copy(got_a[:], board_a[t][:].indirect(l_get_a[:, part]))
+                    else:
+                        nc.scalar.activation(got_a[:], board_a[t][:].indirect(l_get_a[:, part]), COPY)
                     nc.vector.tensor_tensor(
                         diff_hi[h][:, t - 2, :], board_b[t][:].indirect(l_get_b[:, part]), got_a[:], SUBTRACT
                     )
 
         hid_w = []
         hid_s = []
-        for h, tag in enumerate(("ab_sb3", "ab_sb2")):
+        for h, tag in enumerate(("a_hi", "b_hi")):
             reads = slice(HALF * h, HALF * (h + 1))
             hid = sb.tile([P, HALF, PACK], BF16, name="hid%d" % h, tag=tag, align_bytes=64)
             hid_w.append(sb.tile([P, HALF], U32, name="hid_w%d" % h, align_bytes=64))
@@ -198,7 +202,7 @@ def tile_list_oneforboth_twoboards_skip_scattered_kernel(
             nc.scalar.activation(hid[:, :, 2:4], diff_hi[h][:].rearrange("p e o -> p o e"), ABS)
             nc.vector.quantize_mx(out=hid_w[h][:].bitcast(E5M2), scales=hid_s[h][:], in_=hid[:].rearrange("p o t -> p (o t)"))
 
-        page1 = sb.tile([P, PAGE], F32, name="page1", tag="ab_sb3", align_bytes=64)
+        page1 = sb.tile([P, PAGE], F32, name="page1", tag="a_hi", align_bytes=64)
         nc.vector.memset(page1[:], 0.0)
         pages = [page0, page1]
         for h in range(2):

from contextlib import ExitStack

import concourse.mybir as mybir

F32 = mybir.dt.float32
BF16 = mybir.dt.bfloat16
I32 = mybir.dt.int32
U32 = mybir.dt.uint32
U16 = mybir.dt.uint16
U8 = mybir.dt.uint8
E4M3 = mybir.dt.float8_e4m3fn_x4
E5M2 = mybir.dt.float8_e5m2_x4
E2M1 = mybir.dt.float4_e2m1fn_x4
COPY = mybir.ActivationFunctionType.Copy
ABS = mybir.ActivationFunctionType.Abs
SUBTRACT = mybir.AluOpType.subtract

P = 128
PACK = 4
TABLE = 1024
SLOTS = 256
HIDDEN = 512
BOARD = 512
READS = 256
OUTF = 256
PAGE = 1024
HALF = READS // 2
FLOPS = 2 * (2 * 512 * HIDDEN * SLOTS + 2 * 512 * OUTF * READS)


def load_scale_rows(queue, plane, scales, quadrants):
    for q in quadrants:
        rows = scales[0, 4 * q : 4 * q + 4, :].bitcast(I32)
        queue.dma_start(out=plane[32 * q : 32 * q + 32, :].bitcast(I32), in_=rows.partition_broadcast(8))


def as_words(words):
    return words[0].rearrange("p n t -> p (n t)").bitcast(I32)


def tile_list_oneforboth_twoboards_skip_scattered_kernel(
    tc, xt_words, xt_scales, xo_words, xo_scales, w_words, w_scales, wb_words, wb_scales,
    sx_words, sx_scales, ws_words, ws_scales, offs, offs2, offs3, offs4, offs5, offs6, offs7, out,
):
    nc = tc.nc
    with ExitStack() as ctx:
        lists = ctx.enter_context(tc.tile_pool(name="lists", bufs=1))
        sb = ctx.enter_context(tc.tile_pool(name="sb", bufs=1))
        psum = ctx.enter_context(tc.psum_pool(name="psum", bufs=1))

        def list_tile(name):
            return lists.tile([P, SLOTS // 16], U16, name=name)

        l_tok = list_tile("l_tok")
        l_note = list_tile("l_note")
        l_put_a = list_tile("l_put_a")
        l_put_b = list_tile("l_put_b")
        l_get_a = list_tile("l_get_a")
        l_get_b = list_tile("l_get_b")
        l_page = list_tile("l_page")

        xt_w = sb.tile([P, TABLE], U16, name="xt_w")
        xt_s = sb.tile([P, TABLE], U8, name="xt_s")
        xo_w = sb.tile([P, TABLE], U32, name="xo_w")
        xo_s = sb.tile([P, TABLE], U8, name="xo_s")
        w_raw = sb.tile([P, HIDDEN], U32, name="w_raw")
        w_raw_s = sb.tile([P, HIDDEN], U8, name="w_raw_s")
        w_w = sb.tile([P, HIDDEN], U32, name="w_w", align_bytes=64)
        w_s0 = sb.tile([P, P], U8, name="w_s0", align_bytes=64)
        w_s123 = sb.tile([P, HIDDEN - P], U8, name="w_s123", align_bytes=64)
        w_s = [w_s0[:]] + [w_s123[:, P * t : P * (t + 1)] for t in range(PACK - 1)]
        wb_w = sb.tile([P, 2 * OUTF], U8, name="wb_w", align_bytes=64)
        ws_w = sb.tile([P, OUTF], U32, name="ws_w", align_bytes=64)
        sx_w = sb.tile([P, READS], U32, name="sx_w", align_bytes=64)
        planes2 = sb.tile([P, 2 * OUTF + READS], U8, name="planes2", align_bytes=64)
        wb_s = planes2[:, 0:OUTF]
        ws_s = planes2[:, OUTF : 2 * OUTF]
        sx_s = planes2[:, 2 * OUTF :]
        board_a = [sb.tile([P, BOARD], F32, name="board_a%d" % t) for t in range(PACK)]
        board_b = [sb.tile([P, BOARD], F32, name="board_b%d" % t) for t in range(PACK)]


        nc.sync.dma_start(l_tok[:], offs)
        load_scale_rows(nc.scalar, xt_s, xt_scales, (0,))
        load_scale_rows(nc.sync, xt_s, xt_scales, (1,))
        load_scale_rows(nc.scalar, xt_s, xt_scales, (2,))
        nc.sync.dma_start(out=xt_w[:].bitcast(I32), in_=xt_words[0].bitcast(I32))
        load_scale_rows(nc.scalar, xt_s, xt_scales, (3,))
        nc.sync.dma_start(out=w_raw[:].bitcast(I32), in_=as_words(w_words))
        nc.scalar.dma_start(out=xo_w[:].bitcast(I32), in_=as_words(xo_words))
        load_scale_rows(nc.sync, w_raw_s, w_scales, range(4))
        load_scale_rows(nc.gpsimd, xo_s, xo_scales, (2, 3))
        nc.sync.dma_start(l_put_a[:], offs3)
        nc.sync.dma_start(l_note[:], offs2)
        load_scale_rows(nc.sync, xo_s, xo_scales, (0, 1))
        nc.sync.dma_start(l_put_b[:], offs4)
        nc.sync.dma_start(l_get_a[:], offs5)
        nc.sync.dma_start(l_get_b[:], offs6)
        nc.sync.dma_start(out=ws_w[:].bitcast(I32), in_=as_words(ws_words))
        nc.sync.dma_start(out=sx_w[:].bitcast(I32), in_=as_words(sx_words))
        nc.sync.dma_start(out=wb_w[:].bitcast(I32), in_=wb_words[0].bitcast(I32))
        load_scale_rows(nc.sync, ws_s, ws_scales, range(4))
        load_scale_rows(nc.sync, sx_s, sx_scales, range(4))
        load_scale_rows(nc.sync, wb_s, wb_scales, range(4))
        nc.sync.dma_start(l_page[:], offs7)

        tok_w = sb.tile([P, SLOTS], U16, name="tok_w", align_bytes=64)
        tok_s = sb.tile([P, SLOTS], U8, name="tok_s", align_bytes=64)
        note_w = sb.tile([P, SLOTS], U32, name="note_w", align_bytes=64)
        note_s = sb.tile([P, SLOTS], U8, name="note_s", align_bytes=64)

        nc.vector.tensor_copy(tok_w[:], xt_w[:].indirect(l_tok[:]))
        nc.vector.tensor_copy(tok_s[:], xt_s[:].indirect(l_tok[:]))
        nc.vector.tensor_copy(
            w_w[:].rearrange("p (t c i) -> p c t i", t=PACK, i=4),
            w_raw[:].rearrange("p (c i t) -> p c t i", t=PACK, i=4),
        )
        as_loaded = w_raw_s[:].rearrange("p (c i t) -> p c t i", t=PACK, i=16)
        nc.vector.tensor_copy(w_s0[:].rearrange("p (c i) -> p c i", i=16), as_loaded[:, :, 0, :])
        nc.vector.tensor_copy(w_s123[:].rearrange("p (t c i) -> p c t i", t=PACK - 1, i=16), as_loaded[:, :, 1:PACK, :])
        nc.vector.tensor_copy(note_w[:], xo_w[:].indirect(l_note[:]))
        nc.vector.tensor_copy(note_s[:], xo_s[:].indirect(l_note[:]))

        for t in range(PACK):
            nc.vector.memset(board_a[t][:], 0.0)
            nc.vector.memset(board_b[t][:], 0.0)
        page0 = sb.tile([P, PAGE], F32, name="page0")
        nc.vector.memset(page0[:], 0.0)

        def first_stage(acc, t, words, plane):
            cols = slice(P * t, P * (t + 1))
            nc.tensor.matmul_mx(
                out=acc, lhsT=w_w[:, cols].bitcast(E4M3), lhsT_scale=w_s[t],
                rhs=words, rhs_scale=plane, start=True, stop=True,
            )

        acc_a_lo = [psum.tile([P, SLOTS], F32, name="acc_a%d" % t, tag="bank%d" % t) for t in range(2)]
        acc_b_lo = [psum.tile([P, SLOTS], F32, name="acc_b%d" % t) for t in range(2)]
        acc_a_hi = psum.tile([P, 2, SLOTS], F32, name="acc_a_hi")
        acc_b_hi = psum.tile([P, 2, SLOTS], F32, name="acc_b_hi")
        acc_a = [acc[:] for acc in acc_a_lo] + [acc_a_hi[:, e, :] for e in range(2)]
        acc_b = [acc[:] for acc in acc_b_lo] + [acc_b_hi[:, e, :] for e in range(2)]
        for t in range(PACK):
            first_stage(acc_a[t], t, tok_w[:].bitcast(E2M1), tok_s[:])
            first_stage(acc_b[t], t, note_w[:].bitcast(E4M3), note_s[:])

        a_lo_sb = [sb.tile([P, SLOTS], F32, name="a_sb%d" % t) for t in range(2)]
        b_lo_sb = [sb.tile([P, SLOTS], F32, name="b_sb%d" % t) for t in range(2)]
        a_hi_sb = sb.tile([P, 2, SLOTS], F32, name="a_hi_sb", tag="a_hi", align_bytes=64)
        b_hi_sb = sb.tile([P, 2, SLOTS], F32, name="b_hi_sb", tag="b_hi", align_bytes=64)
        a_sb = [x[:] for x in a_lo_sb] + [a_hi_sb[:, e, :] for e in range(2)]
        b_sb = [x[:] for x in b_lo_sb] + [b_hi_sb[:, e, :] for e in range(2)]
        for t in range(2):
            nc.scalar.activation(a_sb[t], acc_a[t], COPY)
            nc.vector.tensor_copy(b_sb[t], acc_b[t])

        acc_p = [
            [psum.tile([P, HALF], F32, name="acc_p%d%d" % (g, h), tag="bank%d" % (2 * h + g)) for h in range(2)]
            for g in range(2)
        ]
        for h in range(2):
            for g in range(2):
                cols = slice(P * g, P * (g + 1))
                reads = slice(HALF * h, HALF * (h + 1))
                nc.tensor.matmul_mx(
                    out=acc_p[g][h][:], lhsT=ws_w[:, cols].bitcast(E4M3), lhsT_scale=ws_s[:, cols],
                    rhs=sx_w[:, reads].bitcast(E4M3), rhs_scale=sx_s[:, reads], start=True, stop=False,
                )

        diff_lo = sb.tile([P, 2, READS], F32, name="diff_lo")
        diff_hi = [sb.tile([P, 2, HALF], F32, name="diff_hi%d" % h) for h in range(2)]
        for t in range(PACK):
            if t == 2:
                nc.scalar.activation(a_hi_sb[:], acc_a_hi[:], COPY)
                nc.vector.tensor_copy(b_hi_sb[:], acc_b_hi[:])
            nc.scalar.activation(board_a[t][:].indirect(l_put_a[:]), a_sb[t], COPY)
            nc.vector.tensor_copy(board_b[t][:].indirect(l_put_b[:]), b_sb[t])
            if t < 2:
                got_a = sb.tile([P, READS], F32, name="got_a%d" % t)
                nc.scalar.activation(got_a[:], board_a[t][:].indirect(l_get_a[:]), COPY)
                nc.vector.tensor_tensor(diff_lo[:, t, :], board_b[t][:].indirect(l_get_b[:]), got_a[:], SUBTRACT)
            else:
                for h in range(2):
                    part = slice(HALF // 16 * h, HALF // 16 * (h + 1))
                    got_a = sb.tile([P, HALF], F32, name="got_a%d%d" % (t, h))
                    if t == 2:
                        nc.vector.tensor_copy(got_a[:], board_a[t][:].indirect(l_get_a[:, part]))
                    else:
                        nc.scalar.activation(got_a[:], board_a[t][:].indirect(l_get_a[:, part]), COPY)
                    nc.vector.tensor_tensor(
                        diff_hi[h][:, t - 2, :], board_b[t][:].indirect(l_get_b[:, part]), got_a[:], SUBTRACT
                    )

        hid_w = []
        hid_s = []
        for h, tag in enumerate(("a_hi", "b_hi")):
            reads = slice(HALF * h, HALF * (h + 1))
            hid = sb.tile([P, HALF, PACK], BF16, name="hid%d" % h, tag=tag, align_bytes=64)
            hid_w.append(sb.tile([P, HALF], U32, name="hid_w%d" % h, align_bytes=64))
            hid_s.append(sb.tile([P, HALF], U8, name="hid_s%d" % h, align_bytes=64))
            nc.scalar.activation(hid[:, :, 0:2], diff_lo[:, :, reads].rearrange("p e o -> p o e"), ABS)
            nc.scalar.activation(hid[:, :, 2:4], diff_hi[h][:].rearrange("p e o -> p o e"), ABS)
            nc.vector.quantize_mx(out=hid_w[h][:].bitcast(E5M2), scales=hid_s[h][:], in_=hid[:].rearrange("p o t -> p (o t)"))

        page1 = sb.tile([P, PAGE], F32, name="page1", tag="a_hi", align_bytes=64)
        nc.vector.memset(page1[:], 0.0)
        pages = [page0, page1]
        for h in range(2):
            for g in range(2):
                nc.tensor.matmul_mx(
                    out=acc_p[g][h][:], lhsT=wb_w[:, 2 * P * g : 2 * P * (g + 1)].bitcast(E2M1),
                    lhsT_scale=wb_s[:, P * g : P * (g + 1)],
                    rhs=hid_w[h][:].bitcast(E5M2), rhs_scale=hid_s[h][:], start=False, stop=True,
                )
        for h in range(2):
            part = slice(HALF // 16 * h, HALF // 16 * (h + 1))
            p_sb = [sb.tile([P, HALF], F32, name="p_sb%d%d" % (g, h)) for g in range(2)]
            nc.scalar.activation(p_sb[0][:], acc_p[0][h][:], COPY)
            nc.scalar.activation(pages[0][:].indirect(l_page[:, part]), p_sb[0][:], COPY)
            nc.vector.tensor_copy(p_sb[1][:], acc_p[1][h][:])
            nc.vector.tensor_copy(pages[1][:].indirect(l_page[:, part]), p_sb[1][:])
        nc.scalar.dma_start(out=out[0:P, :], in_=pages[0][:])
        nc.sync.dma_start(out=out[P : 2 * P, :], in_=pages[1][:])
